import numpy as np
import ml_dtypes


def mxq(x, axis, fmt="e4m3"):
    dtype, down = {"e4m3": (ml_dtypes.float8_e4m3fn, 7), "e5m2": (ml_dtypes.float8_e5m2, 14)}[fmt]
    v = np.moveaxis(np.asarray(x, np.float32).astype(ml_dtypes.bfloat16).astype(np.float64), axis, -1)
    blocks = v.reshape(v.shape[:-1] + (-1, 32))
    amax = np.abs(blocks).max(-1, keepdims=True)
    byte = np.maximum(np.where(amax > 0, np.frexp(amax)[1] - 1 + 127, 0) - down, 1)
    scale = np.exp2(byte - 127.0)
    codes = (blocks / scale).astype(np.float32).astype(dtype).astype(np.float64)
    return np.moveaxis((codes * scale).reshape(v.shape), -1, axis)


WIDE = False


def mx_kscale(k):
    if not WIDE:
        return np.ones(k)
    levels = np.array([10, -10, 5, -5, 0])
    if k % 512:
        return np.exp2(np.random.permutation(np.resize(levels, k // 32))).repeat(32)
    a = np.empty((k // 512, 16))
    for p in range(k // 512):
        a[p, :8] = np.random.permutation(np.resize(levels, 8))
        for g in range(8):
            far = levels[np.abs(levels - a[p, g]) >= 10]
            a[p, g + 8] = far[np.random.randint(len(far))]
    return np.exp2(a.ravel()).repeat(32)


def f64(x):
    return np.asarray(x).astype(np.float64)


def striped(idx):
    return np.tile(idx.reshape(-1, 16).T, (8, 1)).astype(np.uint16)


def unstriped(offs):
    return offs[:16].T.reshape(-1).astype(np.int64)


E2M1 = np.array([0.0, 0.5, 1.0, 1.5, 2.0, 3.0, 4.0, 6.0, -0.0, -0.5, -1.0, -1.5, -2.0, -3.0, -4.0, -6.0])


def pack_weight(w, fmt):
    k, n = w.shape
    w = f64(np.asarray(w, np.float32).astype(ml_dtypes.bfloat16)).reshape(k // 32, 32, n)
    amax = np.abs(w).max(1)
    if fmt == "e4m3":
        byte = np.frexp(amax)[1] - 1 + 127 - 7
    else:
        mant, ex = np.frexp(amax / 6.0)
        byte = np.where(mant > 0.5, ex, ex - 1) + 127
    byte = np.clip(np.where(amax > 0, byte, 1), 1, 254)
    scaled = (w * np.exp2(127.0 - byte)[:, None, :]).reshape(k, n).astype(np.float32)
    by_word = np.ascontiguousarray(scaled.reshape(k // 512, 128, 4, n).transpose(0, 1, 3, 2))
    if fmt == "e4m3":
        words = by_word.astype(ml_dtypes.float8_e4m3fn).view(np.uint8)
    else:
        c = by_word.astype(ml_dtypes.float4_e2m1fn).view(np.uint8) & 0xF
        words = (c[..., 0::2] | (c[..., 1::2] << 4)).reshape(k // 512, 128, 2 * n)
    return np.ascontiguousarray(words), np.ascontiguousarray(byte.astype(np.uint8).reshape(k // 512, 16, n))


def unpack_weight(words, scales, fmt):
    g, _, n = scales.shape
    words = np.ascontiguousarray(words).reshape(g, 128, n, -1)
    if fmt == "e4m3":
        vals = words.view(ml_dtypes.float8_e4m3fn).astype(np.float64)
    else:
        nib = np.empty((g, 128, n, 4), np.uint8)
        nib[..., 0::2] = words & 0xF
        nib[..., 1::2] = words >> 4
        vals = E2M1[nib]
    vals = vals * np.repeat(np.exp2(scales.astype(np.float64) - 127.0), 8, axis=1)[..., None]
    return vals.transpose(0, 1, 3, 2).reshape(g * 512, n)


def silu(v):
    return v / (1.0 + np.exp(-np.maximum(v, -700.0)))


K, T, E, C, H, N = 512, 512, 8, 128, 512, 256


def by_expert(wq, xq):
    return np.concatenate([wq[e].T @ xq[:, e * C:(e + 1) * C] for e in range(E)], axis=1)


def setup_inputs():
    n = np.random.standard_normal
    s = mx_kscale(K)
    u = mx_kscale(H)
    first = np.random.permutation(np.repeat(np.arange(E), T // E))
    second = (first + 1 + np.random.permutation(np.repeat(np.arange(E - 1), -(-T // (E - 1)))[:T])) % E
    while np.bincount(second, minlength=E).max() != T // E:
        load = np.bincount(second, minlength=E); hi, lo = int(load.argmax()), int(load.argmin())
        t = np.flatnonzero((second == hi) & (first != lo))[0]; second[t] = lo
    slot_token = np.empty(E * C, np.int64); pos = np.empty((2, T), np.int64); fill = np.zeros(E, np.int64)
    place = np.stack([np.random.permutation(C) for _ in range(E)])
    for r, deal in enumerate((first, second)):
        for t in np.random.permutation(T):
            e = deal[t]; j = e * C + place[e, fill[e]]; fill[e] += 1; slot_token[j] = t; pos[r, t] = j
    g = np.random.uniform(0.2, 0.8, T)
    x = pack_weight(n((K, T)) * s[:, None], "e4m3")
    w1 = pack_weight(n((K, H)) / np.sqrt(K) / s[:, None] * u, "e2m1")
    w2 = [pack_weight(m, "e4m3") for m in n((E, H, N)) / np.sqrt(H) / u[None, :, None]]
    return {
        "x_words": x[0],
        "x_scales": x[1],
        "w1_words": w1[0],
        "w1_scales": w1[1],
        "w2_words": np.stack([m[0] for m in w2]),
        "w2_scales": np.stack([m[1] for m in w2]),
        "gate": np.stack([np.tile(g, (128, 1)), np.tile(1.0 - g, (128, 1))]).astype(np.float32),
        "offs": striped(slot_token),
        "pos1": striped(pos[0]),
        "pos2": striped(pos[1]),
    }


def reference(x_words, x_scales, w1_words, w1_scales, w2_words, w2_scales, gate, offs, pos1, pos2):
    w1 = unpack_weight(w1_words, w1_scales, "e2m1")
    w2 = np.stack([unpack_weight(w2_words[e], w2_scales[e], "e4m3") for e in range(E)])
    idx = unstriped(offs)
    x = unpack_weight(x_words, x_scales, "e4m3")
    h = silu(w1.T @ x)
    y = by_expert(w2, mxq(h[:, idx], 0, "e4m3"))
    out = sum(f64(gate[r, :1]) * y[:, unstriped(p)] for r, p in enumerate((pos1, pos2)))
    return out

@@ -1,0 +1,179 @@
+from contextlib import ExitStack
+
+import concourse.mybir as mybir
+
+K, T, E, C, H, N = 512, 512, 8, 128, 512, 256
+S = E * C
+P = 128
+FLOPS = 2 * K * H * T + 2 * H * N * S
+
+F32 = mybir.dt.float32
+BF16 = mybir.dt.bfloat16
+I32 = mybir.dt.int32
+U32 = mybir.dt.uint32
+U16 = mybir.dt.uint16
+U8 = mybir.dt.uint8
+FP8X4 = mybir.dt.float8_e4m3fn_x4
+FP4X4 = mybir.dt.float4_e2m1fn_x4
+SILU = mybir.ActivationFunctionType.Silu
+MULT = mybir.AluOpType.mult
+ADD = mybir.AluOpType.add
+
+CHUNKS = (256, 256, 256, 128, 128)
+
+
+def quadrant_rows(scales, q):
+    return scales[0, 4 * q : 4 * q + 4, :].bitcast(I32)
+
+
+def tile_moe_sup_lin_silu_kernel(tc, x_words, x_scales, w1_words, w1_scales, w2_words, w2_scales, gate, offs, pos1, pos2, out):
+    nc = tc.nc
+    with ExitStack() as ctx:
+        keep = ctx.enter_context(tc.tile_pool(name="keep", bufs=1))
+        psum = ctx.enter_context(tc.psum_pool(name="psum", bufs=1))
+
+        w1_raw = keep.tile([P, 2 * H], U8, align_bytes=64)
+        w1s_raw = keep.tile([P, H], U8, align_bytes=64)
+        x_codes = keep.tile([P, T], U32, align_bytes=64)
+        x_plane = keep.tile([P, T], U8, align_bytes=64)
+        nc.vector.memset(x_plane[:].bitcast(I32), 0)
+
+        def load_w1_scales(queue, q):
+            rows = quadrant_rows(w1_scales, q)
+            queue.dma_start(w1s_raw[32 * q : 32 * q + 32].bitcast(I32), rows.unsqueeze(0).broadcast_to([8, 4, H // 4]))
+
+        def load_x_scales(queue, q):
+            queue.dma_start(x_plane[32 * q : 32 * q + 4].bitcast(I32), quadrant_rows(x_scales, q))
+
+        load_w1_scales(nc.sync, 0)
+        load_w1_scales(nc.scalar, 1)
+        nc.sync.dma_start(w1_raw[:].bitcast(I32), w1_words[0].bitcast(I32))
+        load_w1_scales(nc.scalar, 2)
+        nc.sync.dma_start(x_codes[:].bitcast(I32), x_words[0].rearrange("p t d -> p (t d)").bitcast(I32))
+        load_w1_scales(nc.scalar, 3)
+        load_x_scales(nc.sync, 0)
+        load_x_scales(nc.scalar, 1)
+        load_x_scales(nc.sync, 2)
+        load_x_scales(nc.sync, 3)
+
+        offs_t = keep.tile([P, S // 16], U16)
+        nc.sync.dma_start(offs_t[:], offs)
+
+        w2_plane = keep.tile([P, E, N], U8, align_bytes=64)
+        nc.vector.memset(w2_plane[:].rearrange("p e n -> p (e n)").bitcast(I32), 0)
+        w2_codes = keep.tile([P, E, N], U32, align_bytes=64)
+        w2_src = w2_words.rearrange("e s p n d -> p (e s) (n d)").bitcast(I32)
+        w2s_src = w2_scales.rearrange("e s b n -> b (e s) n").bitcast(I32)
+        nc.sync.dma_start(w2_codes[:, 0:4, :].bitcast(I32), w2_src[:, 0:4, :])
+        for q in range(4):
+            nc.sync.dma_start(w2_plane[32 * q : 32 * q + 4].bitcast(I32), w2s_src[4 * q : 4 * q + 4])
+        nc.sync.dma_start(w2_codes[:, 4:8, :].bitcast(I32), w2_src[:, 4:8, :])
+        pos_t = []
+        for r, pos in enumerate((pos1, pos2)):
+            pos_t.append(keep.tile([P, T // 16], U16, name=f"pos{r}"))
+            nc.sync.dma_start(pos_t[r][:], pos)
+        gate_t = keep.tile([P, 2, T], F32)
+        nc.sync.dma_start(gate_t[:], gate.rearrange("r p t -> p r t"))
+
+        w1_codes = keep.tile([P, 2 * H], U8, align_bytes=64)
+        w1_plane = keep.tile([P, H], U8, align_bytes=64)
+        h_pairs = []
+        for a in range(2):
+            js = slice(2 * a, 2 * a + 2)
+            nc.vector.tensor_copy(
+                w1_codes[:].bitcast(U16).rearrange("p (j m) -> p j m", j=4)[:, js, :],
+                w1_raw[:].bitcast(U16).rearrange("p (m j) -> p j m", j=4)[:, js, :],
+            )
+            nc.vector.tensor_copy(
+                w1_plane[:].rearrange("p (j m) -> p j m", j=4)[:, js, :],
+                w1s_raw[:].rearrange("p (m j) -> p j m", j=4)[:, js, :],
+            )
+        for a in range(2):
+            pairs = keep.tile([P, T, 2], BF16, name=f"h_pairs{a}")
+            h_pairs.append(pairs)
+            for t0 in range(0, T, 256):
+                toks = slice(t0, t0 + 256)
+                bank = psum.tile([P, 2, 256], F32, tag=f"bank{2 * a + t0 // 256}", name="bank")
+                for b in range(2):
+                    j = 2 * a + b
+                    nc.tensor.matmul_mx(
+                        out=bank[:, b, :],
+                        lhsT=w1_codes[:, 2 * P * j : 2 * P * (j + 1)].bitcast(FP4X4),
+                        lhsT_scale=w1_plane[:, P * j : P * (j + 1)],
+                        rhs=x_codes[:, toks].bitcast(FP8X4),
+                        rhs_scale=x_plane[:, toks],
+                        start=True,
+                        stop=True,
+                    )
+                nc.scalar.activation(pairs[:, toks, :], bank[:].rearrange("p b t -> p t b"), SILU)
+        windows = [pairs[:].rearrange("p t b -> p (t b)").bitcast(U32) for pairs in h_pairs]
+
+        GATHER = 256
+        picked = [keep.tile([P, 2, GATHER], U32, name=f"picked{c}") for c in range(S // GATHER)]
+        grouped = keep.tile([P, S, 2], U32, align_bytes=64)
+        h_codes = keep.tile([P, S], U32, align_bytes=64)
+        h_plane = keep.tile([P, S], U8, align_bytes=64)
+        y = [keep.tile([P, S], F32, name=f"y{u}") for u in range(2)]
+
+        def gather(c, a):
+            s0 = c * GATHER
+            nc.vector.tensor_copy(picked[c][:, a, :], windows[a].indirect(offs_t[:, s0 // 16 : (s0 + GATHER) // 16]))
+            if a == 1:
+                nc.scalar.copy(grouped[:, s0 : s0 + GATHER, :], picked[c][:].rearrange("p a n -> p n a"))
+
+        def experts(s0, n, u, tag, copy):
+            bank = psum.tile([P, 512], F32, tag=tag, name="bank")
+            for s in range(s0, s0 + n, C):
+                e = s // C
+                nc.tensor.matmul_mx(
+                    out=bank[:, s - s0 : s - s0 + C],
+                    lhsT=w2_codes[:, e, P * u : P * (u + 1)].bitcast(FP8X4),
+                    lhsT_scale=w2_plane[:, e, P * u : P * (u + 1)],
+                    rhs=h_codes[:, s : s + C].bitcast(FP8X4),
+                    rhs_scale=h_plane[:, s : s + C],
+                    start=True,
+                    stop=True,
+                )
+            copy(y[u][:, s0 : s0 + n], bank[:, 0:n])
+
+        gather(0, 0)
+        gather(1, 0)
+        gather(0, 1)
+        gather(1, 1)
+        for c in (2, 3):
+            gather(c, 0)
+            gather(c, 1)
+        s0 = 0
+        for n in CHUNKS:
+            nc.vector.quantize_mx(
+                out=h_codes[:, s0 : s0 + n].bitcast(FP8X4),
+                scales=h_plane[:, s0 : s0 + n],
+                in_=grouped[:, s0 : s0 + n, :].rearrange("p n a -> p (n a)").bitcast(BF16),
+            )
+            s0 += n
+        s0 = 0
+        for c, n in enumerate(CHUNKS):
+            experts(s0, n, 0, f"bank{(4 + c) % 8}", nc.vector.tensor_copy if c in (2, 4) else nc.scalar.copy)
+            s0 += n
+        experts(0, 512, 1, "bank6", nc.scalar.copy)
+        experts(512, 512, 1, "bank7", nc.scalar.copy)
+
+        prod = [[keep.tile([P, T], F32, name=f"prod{u}{r}") for r in range(2)] for u in range(2)]
+        res = [keep.tile([P, T], F32, name=f"res{u}") for u in range(2)]
+
+        def pick(u, r, t0, t1):
+            o = pos_t[r][:, t0 // 16 : t1 // 16]
+            nc.vector.tensor_tensor(prod[u][r][:, t0:t1], y[u][:].indirect(o), gate_t[:, r, t0:t1], MULT)
+
+        def add(u, t0, t1, queue):
+            nc.vector.tensor_tensor(res[u][:, t0:t1], prod[u][0][:, t0:t1], prod[u][1][:, t0:t1], ADD)
+            queue.dma_start(out[P * u : P * (u + 1), t0:t1], res[u][:, t0:t1])
+
+        pick(0, 0, 0, T)
+        pick(0, 1, 0, T)
+        pick(1, 0, 0, T)
+        add(0, 0, T, nc.sync)
+        pick(1, 1, 0, 384)
+        pick(1, 1, 384, T)
+        add(1, 0, 384, nc.sync)
+        add(1, 384, T, nc.scalar)

@@ -1,6 +1,7 @@
 from contextlib import ExitStack
 
 import concourse.mybir as mybir
+from concourse.masks import make_identity
 
 K, T, E, C, H, N = 512, 512, 8, 128, 512, 256
 S = E * C
@@ -88,16 +89,18 @@ def tile_moe_sup_lin_silu_kernel(tc, x_words, x_scales, w1_words, w1_scales, w2_
                 w1_plane[:].rearrange("p (j m) -> p j m", j=4)[:, js, :],
                 w1s_raw[:].rearrange("p (m j) -> p j m", j=4)[:, js, :],
             )
-        for a in range(2):
+        banks_used = 0
+        for a, width in enumerate((128, 256)):
             pairs = keep.tile([P, T, 2], BF16, name=f"h_pairs{a}")
             h_pairs.append(pairs)
-            for t0 in range(0, T, 256):
-                toks = slice(t0, t0 + 256)
-                bank = psum.tile([P, 2, 256], F32, tag=f"bank{2 * a + t0 // 256}", name="bank")
+            for t0 in range(0, T, width):
+                toks = slice(t0, t0 + width)
+                bank = psum.tile([P, 512], F32, tag=f"bank{banks_used}", name="bank")
+                banks_used += 1
                 for b in range(2):
                     j = 2 * a + b
                     nc.tensor.matmul_mx(
-                        out=bank[:, b, :],
+                        out=bank[:, b * width : (b + 1) * width],
                         lhsT=w1_codes[:, 2 * P * j : 2 * P * (j + 1)].bitcast(FP4X4),
                         lhsT_scale=w1_plane[:, P * j : P * (j + 1)],
                         rhs=x_codes[:, toks].bitcast(FP8X4),
@@ -105,7 +108,7 @@ def tile_moe_sup_lin_silu_kernel(tc, x_words, x_scales, w1_words, w1_scales, w2_
                         start=True,
                         stop=True,
                     )
-                nc.scalar.activation(pairs[:, toks, :], bank[:].rearrange("p b t -> p t b"), SILU)
+                nc.scalar.activation(pairs[:, toks, :], bank[:, 0 : 2 * width].rearrange("p (b t) -> p t b", b=2), SILU)
         windows = [pairs[:].rearrange("p t b -> p (t b)").bitcast(U32) for pairs in h_pairs]
 
         GATHER = 256
@@ -153,10 +156,10 @@ def tile_moe_sup_lin_silu_kernel(tc, x_words, x_scales, w1_words, w1_scales, w2_
             s0 += n
         s0 = 0
         for c, n in enumerate(CHUNKS):
-            experts(s0, n, 0, f"bank{(4 + c) % 8}", nc.vector.tensor_copy if c in (2, 4) else nc.scalar.copy)
+            experts(s0, n, 0, f"bank{(6 + c) % 8}", nc.vector.tensor_copy if c in (2, 4) else nc.scalar.copy)
             s0 += n
-        experts(0, 512, 1, "bank6", nc.scalar.copy)
-        experts(512, 512, 1, "bank7", nc.scalar.copy)
+        experts(0, 512, 1, "bank0", nc.scalar.copy)
+        experts(512, 512, 1, "bank1", nc.scalar.copy)
 
         prod = [[keep.tile([P, T], F32, name=f"prod{u}{r}") for r in range(2)] for u in range(2)]
         res = [keep.tile([P, T], F32, name=f"res{u}") for u in range(2)]
@@ -169,11 +172,31 @@ def tile_moe_sup_lin_silu_kernel(tc, x_words, x_scales, w1_words, w1_scales, w2_
             nc.vector.tensor_tensor(res[u][:, t0:t1], prod[u][0][:, t0:t1], prod[u][1][:, t0:t1], ADD)
             queue.dma_start(out[P * u : P * (u + 1), t0:t1], res[u][:, t0:t1])
 
-        pick(0, 0, 0, T)
-        pick(0, 1, 0, T)
+        ident = keep.tile([P, P], F32)
+        make_identity(nc, ident[:])
+
+        def add_turned(t0, tags):
+            turned = psum.tile([P, 512], F32, tag=tags[0], name="bank")
+            for b in range(2):
+                toks = slice(t0 + P * b, t0 + P * (b + 1))
+                for r in range(2):
+                    nc.tensor.matmul(turned[:, P * b : P * (b + 1)], prod[0][r][:, toks], ident[:], start=(r == 0), stop=(r == 1), is_transpose=True)
+            staged = keep.tile([P, 256], F32, name=f"staged{t0}")
+            nc.scalar.copy(staged[:], turned[:, 0:256])
+            back = psum.tile([P, 512], F32, tag=tags[1], name="bank")
+            for b in range(2):
+                nc.tensor.transpose(back[:, P * b : P * (b + 1)], staged[:, P * b : P * (b + 1)], ident[:])
+            nc.scalar.copy(res[0][:, t0 : t0 + 256], back[:, 0:256])
+            nc.scalar.dma_start(out[0:P, t0 : t0 + 256], res[0][:, t0 : t0 + 256])
+
+        for t0, tags in ((0, ("bank3", "bank4")), (256, ("bank5", "bank6"))):
+            pick(0, 0, t0, t0 + 256)
+            pick(0, 1, t0, t0 + 256)
+            add_turned(t0, tags)
         pick(1, 0, 0, T)
-        add(0, 0, T, nc.sync)
-        pick(1, 1, 0, 384)
+        pick(1, 1, 0, 256)
+        pick(1, 1, 256, 384)
+        add(1, 0, 256, nc.sync)
         pick(1, 1, 384, T)
-        add(1, 0, 384, nc.sync)
-        add(1, 384, T, nc.scalar)
+        add(1, 256, 384, nc.sync)
+        add(1, 384, T, nc.sync)

@@ -156,7 +156,7 @@ def tile_moe_sup_lin_silu_kernel(tc, x_words, x_scales, w1_words, w1_scales, w2_
             s0 += n
         s0 = 0
         for c, n in enumerate(CHUNKS):
-            experts(s0, n, 0, f"bank{(6 + c) % 8}", nc.vector.tensor_copy if c in (2, 4) else nc.scalar.copy)
+            experts(s0, n, 0, f"bank{(6 + c) % 8}", nc.vector.tensor_copy if c == 2 else nc.scalar.copy)
             s0 += n
         experts(0, 512, 1, "bank0", nc.scalar.copy)
         experts(512, 512, 1, "bank1", nc.scalar.copy)

@@ -17,10 +17,14 @@ U8 = mybir.dt.uint8
 FP8X4 = mybir.dt.float8_e4m3fn_x4
 FP4X4 = mybir.dt.float4_e2m1fn_x4
 SILU = mybir.ActivationFunctionType.Silu
+COPY = mybir.ActivationFunctionType.Copy
 MULT = mybir.AluOpType.mult
 ADD = mybir.AluOpType.add
 
 CHUNKS = (256, 256, 256, 128, 128)
+FIRST_PAIR = (352, 352)
+SECOND_PAIR = (384, 256, 256, 128)
+WEAVES = (256, 256, 256, 128, 128)
 
 
 def quadrant_rows(scales, q):
@@ -90,6 +94,7 @@ def tile_moe_sup_lin_silu_kernel(tc, x_words, x_scales, w1_words, w1_scales, w2_
                 w1s_raw[:].rearrange("p (m j) -> p j m", j=4)[:, js, :],
             )
         banks_used = 0
+        planes = keep.tile([P, 2, T], BF16, name="planes")
         for a, width in enumerate((128, 256)):
             pairs = keep.tile([P, T, 2], BF16, name=f"h_pairs{a}")
             h_pairs.append(pairs)
@@ -109,20 +114,24 @@ def tile_moe_sup_lin_silu_kernel(tc, x_words, x_scales, w1_words, w1_scales, w2_
                         stop=True,
                     )
                 nc.scalar.activation(pairs[:, toks, :], bank[:, 0 : 2 * width].rearrange("p (b t) -> p t b", b=2), SILU)
+                if a == 0 and t0 + width < T:
+                    nc.vector.tensor_copy(planes[:, :, toks], pairs[:, toks, :].rearrange("p t b -> p b t"))
         windows = [pairs[:].rearrange("p t b -> p (t b)").bitcast(U32) for pairs in h_pairs]
 
-        GATHER = 256
-        picked = [keep.tile([P, 2, GATHER], U32, name=f"picked{c}") for c in range(S // GATHER)]
+        picked = keep.tile([P, 2 * S], U32, name="picked")
         grouped = keep.tile([P, S, 2], U32, align_bytes=64)
         h_codes = keep.tile([P, S], U32, align_bytes=64)
         h_plane = keep.tile([P, S], U8, align_bytes=64)
         y = [keep.tile([P, S], F32, name=f"y{u}") for u in range(2)]
 
-        def gather(c, a):
-            s0 = c * GATHER
-            nc.vector.tensor_copy(picked[c][:, a, :], windows[a].indirect(offs_t[:, s0 // 16 : (s0 + GATHER) // 16]))
-            if a == 1:
-                nc.scalar.copy(grouped[:, s0 : s0 + GATHER, :], picked[c][:].rearrange("p a n -> p n a"))
+        def slots(s0, n):
+            return offs_t[:, s0 // 16 : (s0 + n) // 16]
+
+        def gather(a, s0, n):
+            nc.vector.tensor_copy(picked[:, a * S + s0 : a * S + s0 + n], windows[a].indirect(slots(s0, n)))
+
+        def interleave(s0, n):
+            nc.scalar.copy(grouped[:, s0 : s0 + n, :], picked[:].rearrange("p (a n) -> p n a", a=2)[:, s0 : s0 + n, :])
 
         def experts(s0, n, u, tag, copy):
             bank = psum.tile([P, 512], F32, tag=tag, name="bank")
@@ -139,13 +148,23 @@ def tile_moe_sup_lin_silu_kernel(tc, x_words, x_scales, w1_words, w1_scales, w2_
                 )
             copy(y[u][:, s0 : s0 + n], bank[:, 0:n])
 
-        gather(0, 0)
-        gather(1, 0)
-        gather(0, 1)
-        gather(1, 1)
-        for c in (2, 3):
-            gather(c, 0)
-            gather(c, 1)
+        gather(0, 0, FIRST_PAIR[0])
+        nc.vector.tensor_copy(planes[:, :, T - P : T], h_pairs[0][:, T - P : T, :].rearrange("p t b -> p b t"))
+        s0 = FIRST_PAIR[0]
+        for n in FIRST_PAIR[1:]:
+            gather(0, s0, n)
+            s0 += n
+        halves = picked[:, s0:S].bitcast(BF16).rearrange("p (n b) -> p n b", b=2)
+        for b in range(2):
+            nc.scalar.activation(halves[:, :, b], planes[:, b, :].indirect(slots(s0, S - s0)), COPY)
+        s0 = 0
+        for n in SECOND_PAIR:
+            gather(1, s0, n)
+            s0 += n
+        s0 = 0
+        for n in WEAVES:
+            interleave(s0, n)
+            s0 += n
         s0 = 0
         for n in CHUNKS:
             nc.vector.quantize_mx(

@@ -22,8 +22,8 @@ MULT = mybir.AluOpType.mult
 ADD = mybir.AluOpType.add
 
 CHUNKS = (256, 256, 256, 128, 128)
-FIRST_PAIR = (352, 352)
-SECOND_PAIR = (384, 256, 256, 128)
+FIRST_PAIR = (320, 320)
+SECOND_PAIR = (256, 256, 256, 256)
 WEAVES = (256, 256, 256, 128, 128)
 
 
@@ -131,7 +131,8 @@ def tile_moe_sup_lin_silu_kernel(tc, x_words, x_scales, w1_words, w1_scales, w2_
             nc.vector.tensor_copy(picked[:, a * S + s0 : a * S + s0 + n], windows[a].indirect(slots(s0, n)))
 
         def interleave(s0, n):
-            nc.scalar.copy(grouped[:, s0 : s0 + n, :], picked[:].rearrange("p (a n) -> p n a", a=2)[:, s0 : s0 + n, :])
+            copy = nc.gpsimd.tensor_copy if s0 == 0 else nc.scalar.copy
+            copy(grouped[:, s0 : s0 + n, :], picked[:].rearrange("p (a n) -> p n a", a=2)[:, s0 : s0 + n, :])
 
         def experts(s0, n, u, tag, copy):
             bank = psum.tile([P, 512], F32, tag=tag, name="bank")
@@ -149,7 +150,7 @@ def tile_moe_sup_lin_silu_kernel(tc, x_words, x_scales, w1_words, w1_scales, w2_
             copy(y[u][:, s0 : s0 + n], bank[:, 0:n])
 
         gather(0, 0, FIRST_PAIR[0])
-        nc.vector.tensor_copy(planes[:, :, T - P : T], h_pairs[0][:, T - P : T, :].rearrange("p t b -> p b t"))
+        nc.gpsimd.tensor_copy(planes[:, :, T - P : T], h_pairs[0][:, T - P : T, :].rearrange("p t b -> p b t"))
         s0 = FIRST_PAIR[0]
         for n in FIRST_PAIR[1:]:
             gather(0, s0, n)

@@ -25,6 +25,7 @@ CHUNKS = (256, 256, 256, 128, 128)
 FIRST_PAIR = (320, 320)
 SECOND_PAIR = (256, 256, 256, 256)
 WEAVES = (256, 256, 256, 128, 128)
+TURNED = 128
 
 
 def quadrant_rows(scales, q):
@@ -79,6 +80,10 @@ def tile_moe_sup_lin_silu_kernel(tc, x_words, x_scales, w1_words, w1_scales, w2_
             nc.sync.dma_start(pos_t[r][:], pos)
         gate_t = keep.tile([P, 2, T], F32)
         nc.sync.dma_start(gate_t[:], gate.rearrange("r p t -> p r t"))
+        gate_col = [keep.tile([P, TURNED // P], F32, name=f"gate_col{r}") for r in range(2)]
+        with nc.allow_non_contiguous_dma(reason="one gate value a partition"):
+            for r in range(2):
+                nc.sync.dma_start(gate_col[r][:], gate[r, 0, 0:TURNED].rearrange("(c p) -> p c", p=P))
 
         w1_codes = keep.tile([P, 2 * H], U8, align_bytes=64)
         w1_plane = keep.tile([P, H], U8, align_bytes=64)
@@ -178,45 +183,65 @@ def tile_moe_sup_lin_silu_kernel(tc, x_words, x_scales, w1_words, w1_scales, w2_
         for c, n in enumerate(CHUNKS):
             experts(s0, n, 0, f"bank{(6 + c) % 8}", nc.vector.tensor_copy if c == 2 else nc.scalar.copy)
             s0 += n
-        experts(0, 512, 1, "bank0", nc.scalar.copy)
-        experts(512, 512, 1, "bank1", nc.scalar.copy)
 
         prod = [[keep.tile([P, T], F32, name=f"prod{u}{r}") for r in range(2)] for u in range(2)]
         res = [keep.tile([P, T], F32, name=f"res{u}") for u in range(2)]
-
-        def pick(u, r, t0, t1):
-            o = pos_t[r][:, t0 // 16 : t1 // 16]
-            nc.vector.tensor_tensor(prod[u][r][:, t0:t1], y[u][:].indirect(o), gate_t[:, r, t0:t1], MULT)
-
-        def add(u, t0, t1, queue):
-            nc.vector.tensor_tensor(res[u][:, t0:t1], prod[u][0][:, t0:t1], prod[u][1][:, t0:t1], ADD)
-            queue.dma_start(out[P * u : P * (u + 1), t0:t1], res[u][:, t0:t1])
-
         ident = keep.tile([P, P], F32)
         make_identity(nc, ident[:])
 
-        def add_turned(t0, tags):
-            turned = psum.tile([P, 512], F32, tag=tags[0], name="bank")
-            for b in range(2):
-                toks = slice(t0 + P * b, t0 + P * (b + 1))
-                for r in range(2):
-                    nc.tensor.matmul(turned[:, P * b : P * (b + 1)], prod[0][r][:, toks], ident[:], start=(r == 0), stop=(r == 1), is_transpose=True)
-            staged = keep.tile([P, 256], F32, name=f"staged{t0}")
-            nc.scalar.copy(staged[:], turned[:, 0:256])
-            back = psum.tile([P, 512], F32, tag=tags[1], name="bank")
-            for b in range(2):
-                nc.tensor.transpose(back[:, P * b : P * (b + 1)], staged[:, P * b : P * (b + 1)], ident[:])
-            nc.scalar.copy(res[0][:, t0 : t0 + 256], back[:, 0:256])
-            nc.scalar.dma_start(out[0:P, t0 : t0 + 256], res[0][:, t0 : t0 + 256])
+        def tokens(r, t0, t1):
+            return pos_t[r][:, t0 // 16 : t1 // 16]
 
-        for t0, tags in ((0, ("bank3", "bank4")), (256, ("bank5", "bank6"))):
-            pick(0, 0, t0, t0 + 256)
-            pick(0, 1, t0, t0 + 256)
-            add_turned(t0, tags)
-        pick(1, 0, 0, T)
-        pick(1, 1, 0, 256)
-        pick(1, 1, 256, 384)
-        add(1, 0, 256, nc.sync)
+        def pick(u, r, t0, t1):
+            nc.vector.tensor_tensor(prod[u][r][:, t0:t1], y[u][:].indirect(tokens(r, t0, t1)), gate_t[:, r, t0:t1], MULT)
+
+        def add(u, t0, t1):
+            nc.vector.tensor_tensor(res[u][:, t0:t1], prod[u][0][:, t0:t1], prod[u][1][:, t0:t1], ADD)
+            nc.sync.dma_start(out[P * u : P * (u + 1), t0:t1], res[u][:, t0:t1])
+
+        plain = [[keep.tile([P, P], F32, name=f"plain{u}{r}") for r in range(2)] for u in range(2)]
+        weighed = [[keep.tile([P, P], F32, name=f"weighed{u}{r}") for r in range(2)] for u in range(2)]
+        turned = {}
+        back = {}
+
+        def fetch(u):
+            for r in range(2):
+                nc.scalar.activation(plain[u][r][:], y[u][:].indirect(tokens(r, 0, P)), COPY)
+
+        def turn(u):
+            for r in range(2):
+                turned[u, r] = psum.tile([P, 512], F32, tag=f"bank{2 + 2 * u + r}", name="bank")
+                nc.tensor.transpose(turned[u, r][:, 0:P], plain[u][r][:], ident[:])
+
+        def weigh(u):
+            for r in range(2):
+                nc.scalar.activation(weighed[u][r][:], turned[u, r][:, 0:P], COPY, scale=gate_col[r][:, 0:1])
+            back[u] = psum.tile([P, 512], F32, tag=f"bank{6 + u}", name="bank")
+            for r in range(2):
+                nc.tensor.matmul(back[u][:, 0:P], weighed[u][r][:], ident[:], start=(r == 0), stop=(r == 1), is_transpose=True)
+
+        def leave(u):
+            nc.scalar.copy(res[u][:, 0:P], back[u][:, 0:P])
+            nc.scalar.dma_start(out[P * u : P * (u + 1), 0:P], res[u][:, 0:P])
+
+        fetch(0)
+        experts(0, 512, 1, "bank0", nc.scalar.copy)
+        experts(512, 512, 1, "bank1", nc.scalar.copy)
+        turn(0)
+        fetch(1)
+        turn(1)
+        weigh(0)
+        weigh(1)
+        leave(0)
+        leave(1)
+
+        pick(0, 0, P, T)
+        pick(0, 1, P, 320)
+        pick(0, 1, 320, T)
+        add(0, P, 320)
+        pick(1, 0, P, T)
+        add(0, 320, T)
+        pick(1, 1, P, 384)
         pick(1, 1, 384, T)
-        add(1, 256, 384, nc.sync)
-        add(1, 384, T, nc.sync)
+        add(1, P, 384)
+        add(1, 384, T)

@@ -22,10 +22,9 @@ MULT = mybir.AluOpType.mult
 ADD = mybir.AluOpType.add
 
 CHUNKS = (256, 256, 256, 128, 128)
+STARTS = (0, 256, 512, 768, 896)
 FIRST_PAIR = (320, 320)
-SECOND_PAIR = (256, 256, 256, 256)
-WEAVES = (256, 256, 256, 128, 128)
-TURNED = 128
+TURNED = 256
 
 
 def quadrant_rows(scales, q):
@@ -36,6 +35,7 @@ def tile_moe_sup_lin_silu_kernel(tc, x_words, x_scales, w1_words, w1_scales, w2_
     nc = tc.nc
     with ExitStack() as ctx:
         keep = ctx.enter_context(tc.tile_pool(name="keep", bufs=1))
+        shared = ctx.enter_context(tc.tile_pool(name="shared", bufs=1))
         psum = ctx.enter_context(tc.psum_pool(name="psum", bufs=1))
 
         w1_raw = keep.tile([P, 2 * H], U8, align_bytes=64)
@@ -101,7 +101,7 @@ def tile_moe_sup_lin_silu_kernel(tc, x_words, x_scales, w1_words, w1_scales, w2_
         banks_used = 0
         planes = keep.tile([P, 2, T], BF16, name="planes")
         for a, width in enumerate((128, 256)):
-            pairs = keep.tile([P, T, 2], BF16, name=f"h_pairs{a}")
+            pairs = shared.tile([P, T, 2], BF16, name=f"h_pairs{a}", offset=(5120, 0)[a], align_bytes=64)
             h_pairs.append(pairs)
             for t0 in range(0, T, width):
                 toks = slice(t0, t0 + width)
@@ -123,66 +123,92 @@ def tile_moe_sup_lin_silu_kernel(tc, x_words, x_scales, w1_words, w1_scales, w2_
                     nc.vector.tensor_copy(planes[:, :, toks], pairs[:, toks, :].rearrange("p t b -> p b t"))
         windows = [pairs[:].rearrange("p t b -> p (t b)").bitcast(U32) for pairs in h_pairs]
 
-        picked = keep.tile([P, 2 * S], U32, name="picked")
-        grouped = keep.tile([P, S, 2], U32, align_bytes=64)
-        h_codes = keep.tile([P, S], U32, align_bytes=64)
+        GROUPED = S + STARTS[3]
+        work = keep.tile([P, GROUPED + 2 * S], U32, name="work", tag="work", align_bytes=64)
+        h_codes = {}
         h_plane = keep.tile([P, S], U8, align_bytes=64)
-        y = [keep.tile([P, S], F32, name=f"y{u}") for u in range(2)]
+        second_at = [S + STARTS[0], S + STARTS[1], S + STARTS[2], S, S + CHUNKS[3]]
 
         def slots(s0, n):
             return offs_t[:, s0 // 16 : (s0 + n) // 16]
 
-        def gather(a, s0, n):
-            nc.vector.tensor_copy(picked[:, a * S + s0 : a * S + s0 + n], windows[a].indirect(slots(s0, n)))
+        def gather_first(s0, n):
+            nc.vector.tensor_copy(work[:, s0 : s0 + n], windows[0].indirect(slots(s0, n)))
 
-        def interleave(s0, n):
-            copy = nc.gpsimd.tensor_copy if s0 == 0 else nc.scalar.copy
-            copy(grouped[:, s0 : s0 + n, :], picked[:].rearrange("p (a n) -> p n a", a=2)[:, s0 : s0 + n, :])
+        def gather_second(c):
+            nc.vector.tensor_copy(work[:, second_at[c] : second_at[c] + CHUNKS[c]], windows[1].indirect(slots(STARTS[c], CHUNKS[c])))
 
-        def experts(s0, n, u, tag, copy):
-            bank = psum.tile([P, 512], F32, tag=tag, name="bank")
-            for s in range(s0, s0 + n, C):
+        def grouped(c):
+            return work[:, GROUPED + 2 * STARTS[c] : GROUPED + 2 * (STARTS[c] + CHUNKS[c])]
+
+        def interleave(c):
+            copy = nc.gpsimd.tensor_copy if c == 0 else nc.scalar.copy
+            apart = second_at[c] - STARTS[c]
+            both = work[:, STARTS[c] : STARTS[c] + 2 * apart].rearrange("p (a n) -> p n a", a=2)[:, 0 : CHUNKS[c], :]
+            copy(grouped(c).rearrange("p (n a) -> p n a", a=2), both)
+
+        def quantise(c):
+            cols = slice(STARTS[c], STARTS[c] + CHUNKS[c])
+            if c == 2:
+                h_codes[c] = shared.tile([P, CHUNKS[c]], U32, name="late_codes", offset=0, align_bytes=64)
+            else:
+                h_codes[c] = keep.tile([P, CHUNKS[c]], U32, name=f"codes{c}", align_bytes=64)
+            nc.vector.quantize_mx(out=h_codes[c][:].bitcast(FP8X4), scales=h_plane[:, cols], in_=grouped(c).bitcast(BF16))
+
+        def experts(c, u, bank, at):
+            for s in range(STARTS[c], STARTS[c] + CHUNKS[c], C):
                 e = s // C
                 nc.tensor.matmul_mx(
-                    out=bank[:, s - s0 : s - s0 + C],
+                    out=bank[:, s - at : s - at + C],
                     lhsT=w2_codes[:, e, P * u : P * (u + 1)].bitcast(FP8X4),
                     lhsT_scale=w2_plane[:, e, P * u : P * (u + 1)],
-                    rhs=h_codes[:, s : s + C].bitcast(FP8X4),
+                    rhs=h_codes[c][:, s - STARTS[c] : s - STARTS[c] + C].bitcast(FP8X4),
                     rhs_scale=h_plane[:, s : s + C],
                     start=True,
                     stop=True,
                 )
-            copy(y[u][:, s0 : s0 + n], bank[:, 0:n])
 
-        gather(0, 0, FIRST_PAIR[0])
+        gather_first(0, FIRST_PAIR[0])
         nc.gpsimd.tensor_copy(planes[:, :, T - P : T], h_pairs[0][:, T - P : T, :].rearrange("p t b -> p b t"))
-        s0 = FIRST_PAIR[0]
-        for n in FIRST_PAIR[1:]:
-            gather(0, s0, n)
-            s0 += n
-        halves = picked[:, s0:S].bitcast(BF16).rearrange("p (n b) -> p n b", b=2)
+        gather_first(FIRST_PAIR[0], FIRST_PAIR[1])
+        s0 = sum(FIRST_PAIR)
+        halves = work[:, s0:S].bitcast(BF16).rearrange("p (n b) -> p n b", b=2)
         for b in range(2):
             nc.scalar.activation(halves[:, :, b], planes[:, b, :].indirect(slots(s0, S - s0)), COPY)
-        s0 = 0
-        for n in SECOND_PAIR:
-            gather(1, s0, n)
-            s0 += n
-        s0 = 0
-        for n in WEAVES:
-            interleave(s0, n)
-            s0 += n
-        s0 = 0
-        for n in CHUNKS:
-            nc.vector.quantize_mx(
-                out=h_codes[:, s0 : s0 + n].bitcast(FP8X4),
-                scales=h_plane[:, s0 : s0 + n],
-                in_=grouped[:, s0 : s0 + n, :].rearrange("p n a -> p (n a)").bitcast(BF16),
-            )
-            s0 += n
-        s0 = 0
-        for c, n in enumerate(CHUNKS):
-            experts(s0, n, 0, f"bank{(6 + c) % 8}", nc.vector.tensor_copy if c == 2 else nc.scalar.copy)
-            s0 += n
+        for c in range(3):
+            gather_second(c)
+            interleave(c)
+        for c in range(2):
+            quantise(c)
+            gather_second(3 + c)
+            interleave(3 + c)
+        for c in range(2, 5):
+            quantise(c)
+
+        GROUPS = ((0, 1), (2,), (3, 4))
+        y = [shared.tile([P, S], F32, name="y0", offset=1024, align_bytes=64), keep.tile([P, S], F32, name="y1", tag="work", align_bytes=64)]
+        banks = {}
+
+        def products(u, g, tag):
+            banks[u, g] = psum.tile([P, 512], F32, tag=tag, name="bank")
+            for c in GROUPS[g]:
+                experts(c, u, banks[u, g], STARTS[GROUPS[g][0]])
+
+        def empty(u, g):
+            copy = nc.vector.tensor_copy if u == 1 and g < 2 else nc.scalar.copy
+            s0, n = STARTS[GROUPS[g][0]], sum(CHUNKS[c] for c in GROUPS[g])
+            copy(y[u][:, s0 : s0 + n], banks[u, g][:, 0:n])
+
+        products(0, 0, "bank6")
+        products(1, 0, "bank7")
+        products(0, 1, "bank0")
+        products(0, 2, "bank1")
+        for g in range(3):
+            empty(0, g)
+        products(1, 1, "bank2")
+        products(1, 2, "bank3")
+        for g in range(3):
+            empty(1, g)
 
         prod = [[keep.tile([P, T], F32, name=f"prod{u}{r}") for r in range(2)] for u in range(2)]
         res = [keep.tile([P, T], F32, name=f"res{u}") for u in range(2)]
@@ -199,49 +225,47 @@ def tile_moe_sup_lin_silu_kernel(tc, x_words, x_scales, w1_words, w1_scales, w2_
             nc.vector.tensor_tensor(res[u][:, t0:t1], prod[u][0][:, t0:t1], prod[u][1][:, t0:t1], ADD)
             nc.sync.dma_start(out[P * u : P * (u + 1), t0:t1], res[u][:, t0:t1])
 
-        plain = [[keep.tile([P, P], F32, name=f"plain{u}{r}") for r in range(2)] for u in range(2)]
-        weighed = [[keep.tile([P, P], F32, name=f"weighed{u}{r}") for r in range(2)] for u in range(2)]
+        SHARE = (256, 128)
+        plain = [[keep.tile([P, SHARE[u]], F32, name=f"plain{u}{r}") for r in range(2)] for u in range(2)]
+        weighed = [[keep.tile([P, SHARE[u]], F32, name=f"weighed{u}{r}") for r in range(2)] for u in range(2)]
         turned = {}
         back = {}
 
-        def fetch(u):
+        def fetch(u, r):
+            nc.scalar.activation(plain[u][r][:], y[u][:].indirect(tokens(r, 0, SHARE[u])), COPY)
+            turned[u, r] = psum.tile([P, 512], F32, tag=f"bank{2 + 2 * u + r}", name="bank")
+            for t0 in range(0, SHARE[u], P):
+                nc.tensor.transpose(turned[u, r][:, t0 : t0 + P], plain[u][r][:, t0 : t0 + P], ident[:])
+
+        def weigh(u, b, tag):
+            blk = slice(P * b, P * (b + 1))
+            back[u, b] = psum.tile([P, 512], F32, tag=tag, name="bank")
             for r in range(2):
-                nc.scalar.activation(plain[u][r][:], y[u][:].indirect(tokens(r, 0, P)), COPY)
+                nc.scalar.activation(weighed[u][r][:, blk], turned[u, r][:, blk], COPY, scale=gate_col[r][:, b : b + 1])
+                nc.tensor.matmul(back[u, b][:, 0:P], weighed[u][r][:, blk], ident[:], start=(r == 0), stop=(r == 1), is_transpose=True)
 
-        def turn(u):
-            for r in range(2):
-                turned[u, r] = psum.tile([P, 512], F32, tag=f"bank{2 + 2 * u + r}", name="bank")
-                nc.tensor.transpose(turned[u, r][:, 0:P], plain[u][r][:], ident[:])
+        def leave(u, b):
+            blk = slice(P * b, P * (b + 1))
+            nc.scalar.copy(res[u][:, blk], back[u, b][:, 0:P])
+            nc.scalar.dma_start(out[P * u : P * (u + 1), blk], res[u][:, blk])
 
-        def weigh(u):
-            for r in range(2):
-                nc.scalar.activation(weighed[u][r][:], turned[u, r][:, 0:P], COPY, scale=gate_col[r][:, 0:1])
-            back[u] = psum.tile([P, 512], F32, tag=f"bank{6 + u}", name="bank")
-            for r in range(2):
-                nc.tensor.matmul(back[u][:, 0:P], weighed[u][r][:], ident[:], start=(r == 0), stop=(r == 1), is_transpose=True)
+        fetch(0, 0)
+        fetch(0, 1)
+        fetch(1, 0)
+        weigh(0, 0, "bank1")
+        fetch(1, 1)
+        leave(0, 0)
+        weigh(0, 1, "bank7")
+        weigh(1, 0, "bank6")
+        leave(0, 1)
+        leave(1, 0)
 
-        def leave(u):
-            nc.scalar.copy(res[u][:, 0:P], back[u][:, 0:P])
-            nc.scalar.dma_start(out[P * u : P * (u + 1), 0:P], res[u][:, 0:P])
-
-        fetch(0)
-        experts(0, 512, 1, "bank0", nc.scalar.copy)
-        experts(512, 512, 1, "bank1", nc.scalar.copy)
-        turn(0)
-        fetch(1)
-        turn(1)
-        weigh(0)
-        weigh(1)
-        leave(0)
-        leave(1)
-
-        pick(0, 0, P, T)
-        pick(0, 1, P, 320)
-        pick(0, 1, 320, T)
-        add(0, P, 320)
-        pick(1, 0, P, T)
-        add(0, 320, T)
-        pick(1, 1, P, 384)
+        pick(0, 0, SHARE[0], T)
+        pick(0, 1, SHARE[0], T)
+        pick(1, 0, SHARE[1], T)
+        pick(1, 1, SHARE[1], 384)
+        add(0, SHARE[0], 384)
+        add(1, SHARE[1], 384)
         pick(1, 1, 384, T)
-        add(1, P, 384)
+        add(0, 384, T)
         add(1, 384, T)

@@ -78,8 +78,8 @@ def tile_moe_sup_lin_silu_kernel(tc, x_words, x_scales, w1_words, w1_scales, w2_
         for r, pos in enumerate((pos1, pos2)):
             pos_t.append(keep.tile([P, T // 16], U16, name=f"pos{r}"))
             nc.sync.dma_start(pos_t[r][:], pos)
-        gate_t = keep.tile([P, 2, T], F32)
-        nc.sync.dma_start(gate_t[:], gate.rearrange("r p t -> p r t"))
+        gate_t = keep.tile([P, 2, T - P], F32)
+        nc.sync.dma_start(gate_t[:], gate[:, :, P:T].rearrange("r p t -> p r t"))
         gate_col = [keep.tile([P, TURNED // P], F32, name=f"gate_col{r}") for r in range(2)]
         with nc.allow_non_contiguous_dma(reason="one gate value a partition"):
             for r in range(2):
@@ -219,7 +219,7 @@ def tile_moe_sup_lin_silu_kernel(tc, x_words, x_scales, w1_words, w1_scales, w2_
             return pos_t[r][:, t0 // 16 : t1 // 16]
 
         def pick(u, r, t0, t1):
-            nc.vector.tensor_tensor(prod[u][r][:, t0:t1], y[u][:].indirect(tokens(r, t0, t1)), gate_t[:, r, t0:t1], MULT)
+            nc.vector.tensor_tensor(prod[u][r][:, t0:t1], y[u][:].indirect(tokens(r, t0, t1)), gate_t[:, r, t0 - P : t1 - P], MULT)
 
         def add(u, t0, t1):
             nc.vector.tensor_tensor(res[u][:, t0:t1], prod[u][0][:, t0:t1], prod[u][1][:, t0:t1], ADD)

@@ -148,12 +148,17 @@ def tile_moe_sup_lin_silu_kernel(tc, x_words, x_scales, w1_words, w1_scales, w2_
             copy(grouped(c).rearrange("p (n a) -> p n a", a=2), both)
 
         def quantise(c):
-            cols = slice(STARTS[c], STARTS[c] + CHUNKS[c])
             if c == 2:
                 h_codes[c] = shared.tile([P, CHUNKS[c]], U32, name="late_codes", offset=0, align_bytes=64)
             else:
                 h_codes[c] = keep.tile([P, CHUNKS[c]], U32, name=f"codes{c}", align_bytes=64)
-            nc.vector.quantize_mx(out=h_codes[c][:].bitcast(FP8X4), scales=h_plane[:, cols], in_=grouped(c).bitcast(BF16))
+            step = C if c == 2 else CHUNKS[c]
+            for lo in range(0, CHUNKS[c], step):
+                nc.vector.quantize_mx(
+                    out=h_codes[c][:, lo : lo + step].bitcast(FP8X4),
+                    scales=h_plane[:, STARTS[c] + lo : STARTS[c] + lo + step],
+                    in_=grouped(c)[:, 2 * lo : 2 * (lo + step)].bitcast(BF16),
+                )
 
         def experts(c, u, bank, at):
             for s in range(STARTS[c], STARTS[c] + CHUNKS[c], C):

@@ -98,6 +98,17 @@ def tile_moe_sup_lin_silu_kernel(tc, x_words, x_scales, w1_words, w1_scales, w2_
                 w1_plane[:].rearrange("p (j m) -> p j m", j=4)[:, js, :],
                 w1s_raw[:].rearrange("p (m j) -> p j m", j=4)[:, js, :],
             )
+        spare = psum.tile([P, 512], F32, tag="bank7", name="bank")
+        for lo, n in ((0, 256), (256, 128)):
+            nc.tensor.matmul_mx(
+                out=spare[:, lo : lo + n],
+                lhsT=x_codes[:, 0:P].bitcast(FP8X4),
+                lhsT_scale=w1s_raw[:, 0:P],
+                rhs=w1_raw[:, 2 * lo : 2 * (lo + n)].bitcast(FP4X4),
+                rhs_scale=w1s_raw[:, lo : lo + n],
+                start=True,
+                stop=True,
+            )
         banks_used = 0
         planes = keep.tile([P, 2, T], BF16, name="planes")
         for a, width in enumerate((128, 256)):

@@ -23,7 +23,8 @@ ADD = mybir.AluOpType.add
 
 CHUNKS = (256, 256, 256, 128, 128)
 STARTS = (0, 256, 512, 768, 896)
-FIRST_PAIR = (320, 320)
+FIRST_PAIR = 640
+WIDE = 896
 TURNED = 256
 
 
@@ -55,12 +56,10 @@ def tile_moe_sup_lin_silu_kernel(tc, x_words, x_scales, w1_words, w1_scales, w2_
         load_w1_scales(nc.scalar, 1)
         nc.sync.dma_start(w1_raw[:].bitcast(I32), w1_words[0].bitcast(I32))
         load_w1_scales(nc.scalar, 2)
+        load_w1_scales(nc.sync, 3)
         nc.sync.dma_start(x_codes[:].bitcast(I32), x_words[0].rearrange("p t d -> p (t d)").bitcast(I32))
-        load_w1_scales(nc.scalar, 3)
-        load_x_scales(nc.sync, 0)
-        load_x_scales(nc.scalar, 1)
-        load_x_scales(nc.sync, 2)
-        load_x_scales(nc.sync, 3)
+        for q in range(4):
+            load_x_scales(nc.sync, q)
 
         offs_t = keep.tile([P, S // 16], U16)
         nc.sync.dma_start(offs_t[:], offs)
@@ -88,6 +87,7 @@ def tile_moe_sup_lin_silu_kernel(tc, x_words, x_scales, w1_words, w1_scales, w2_
         w1_codes = keep.tile([P, 2 * H], U8, align_bytes=64)
         w1_plane = keep.tile([P, H], U8, align_bytes=64)
         h_pairs = []
+        windows = []
         for a in range(2):
             js = slice(2 * a, 2 * a + 2)
             nc.vector.tensor_copy(
@@ -112,7 +112,9 @@ def tile_moe_sup_lin_silu_kernel(tc, x_words, x_scales, w1_words, w1_scales, w2_
         banks_used = 0
         planes = keep.tile([P, 2, T], BF16, name="planes")
         for a, width in enumerate((128, 256)):
-            pairs = shared.tile([P, T, 2], BF16, name=f"h_pairs{a}", offset=(5120, 0)[a], align_bytes=64)
+            window = shared.tile([P, (WIDE, T)[a]], U32, name=f"window{a}", offset=(5120, 0)[a], align_bytes=64)
+            windows.append(window[:])
+            pairs = window[:, 0:T].bitcast(BF16).rearrange("p (t b) -> p t b", b=2)
             h_pairs.append(pairs)
             for t0 in range(0, T, width):
                 toks = slice(t0, t0 + width)
@@ -132,7 +134,6 @@ def tile_moe_sup_lin_silu_kernel(tc, x_words, x_scales, w1_words, w1_scales, w2_
                 nc.scalar.activation(pairs[:, toks, :], bank[:, 0 : 2 * width].rearrange("p (b t) -> p t b", b=2), SILU)
                 if a == 0 and t0 + width < T:
                     nc.vector.tensor_copy(planes[:, :, toks], pairs[:, toks, :].rearrange("p t b -> p b t"))
-        windows = [pairs[:].rearrange("p t b -> p (t b)").bitcast(U32) for pairs in h_pairs]
 
         GROUPED = S + STARTS[3]
         work = keep.tile([P, GROUPED + 2 * S], U32, name="work", tag="work", align_bytes=64)
@@ -184,10 +185,9 @@ def tile_moe_sup_lin_silu_kernel(tc, x_words, x_scales, w1_words, w1_scales, w2_
                     stop=True,
                 )
 
-        gather_first(0, FIRST_PAIR[0])
+        gather_first(0, FIRST_PAIR)
         nc.gpsimd.tensor_copy(planes[:, :, T - P : T], h_pairs[0][:, T - P : T, :].rearrange("p t b -> p b t"))
-        gather_first(FIRST_PAIR[0], FIRST_PAIR[1])
-        s0 = sum(FIRST_PAIR)
+        s0 = FIRST_PAIR
         halves = work[:, s0:S].bitcast(BF16).rearrange("p (n b) -> p n b", b=2)
         for b in range(2):
             nc.scalar.activation(halves[:, :, b], planes[:, b, :].indirect(slots(s0, S - s0)), COPY)

@@ -278,10 +278,12 @@ def tile_moe_sup_lin_silu_kernel(tc, x_words, x_scales, w1_words, w1_scales, w2_
 
         pick(0, 0, SHARE[0], T)
         pick(0, 1, SHARE[0], T)
-        pick(1, 0, SHARE[1], T)
-        pick(1, 1, SHARE[1], 384)
-        add(0, SHARE[0], 384)
-        add(1, SHARE[1], 384)
-        pick(1, 1, 384, T)
-        add(0, 384, T)
-        add(1, 384, T)
+        pick(1, 0, P, 2 * P)
+        pick(1, 1, P, 2 * P)
+        add(0, SHARE[0], T)
+        add(1, P, 2 * P)
+        pick(1, 0, 2 * P, T)
+        pick(1, 1, 2 * P, 3 * P)
+        pick(1, 1, 3 * P, T)
+        add(1, 2 * P, 3 * P)
+        add(1, 3 * P, T)

from contextlib import ExitStack

import concourse.mybir as mybir
from concourse.masks import make_identity

K, T, E, C, H, N = 512, 512, 8, 128, 512, 256
S = E * C
P = 128
FLOPS = 2 * K * H * T + 2 * H * N * S

F32 = mybir.dt.float32
BF16 = mybir.dt.bfloat16
I32 = mybir.dt.int32
U32 = mybir.dt.uint32
U16 = mybir.dt.uint16
U8 = mybir.dt.uint8
FP8X4 = mybir.dt.float8_e4m3fn_x4
FP4X4 = mybir.dt.float4_e2m1fn_x4
SILU = mybir.ActivationFunctionType.Silu
COPY = mybir.ActivationFunctionType.Copy
MULT = mybir.AluOpType.mult
ADD = mybir.AluOpType.add

CHUNKS = (256, 256, 256, 128, 128)
STARTS = (0, 256, 512, 768, 896)
FIRST_PAIR = 640
WIDE = 896
TURNED = 256


def quadrant_rows(scales, q):
    return scales[0, 4 * q : 4 * q + 4, :].bitcast(I32)


def tile_moe_sup_lin_silu_kernel(tc, x_words, x_scales, w1_words, w1_scales, w2_words, w2_scales, gate, offs, pos1, pos2, out):
    nc = tc.nc
    with ExitStack() as ctx:
        keep = ctx.enter_context(tc.tile_pool(name="keep", bufs=1))
        shared = ctx.enter_context(tc.tile_pool(name="shared", bufs=1))
        psum = ctx.enter_context(tc.psum_pool(name="psum", bufs=1))

        w1_raw = keep.tile([P, 2 * H], U8, align_bytes=64)
        w1s_raw = keep.tile([P, H], U8, align_bytes=64)
        x_codes = keep.tile([P, T], U32, align_bytes=64)
        x_plane = keep.tile([P, T], U8, align_bytes=64)
        nc.vector.memset(x_plane[:].bitcast(I32), 0)

        def load_w1_scales(queue, q):
            rows = quadrant_rows(w1_scales, q)
            queue.dma_start(w1s_raw[32 * q : 32 * q + 32].bitcast(I32), rows.unsqueeze(0).broadcast_to([8, 4, H // 4]))

        def load_x_scales(queue, q):
            queue.dma_start(x_plane[32 * q : 32 * q + 4].bitcast(I32), quadrant_rows(x_scales, q))

        load_w1_scales(nc.sync, 0)
        load_w1_scales(nc.scalar, 1)
        nc.sync.dma_start(w1_raw[:].bitcast(I32), w1_words[0].bitcast(I32))
        load_w1_scales(nc.scalar, 2)
        load_w1_scales(nc.sync, 3)
        nc.sync.dma_start(x_codes[:].bitcast(I32), x_words[0].rearrange("p t d -> p (t d)").bitcast(I32))
        for q in range(4):
            load_x_scales(nc.sync, q)

        offs_t = keep.tile([P, S // 16], U16)
        nc.sync.dma_start(offs_t[:], offs)

        w2_plane = keep.tile([P, E, N], U8, align_bytes=64)
        nc.vector.memset(w2_plane[:].rearrange("p e n -> p (e n)").bitcast(I32), 0)
        w2_codes = keep.tile([P, E, N], U32, align_bytes=64)
        w2_src = w2_words.rearrange("e s p n d -> p (e s) (n d)").bitcast(I32)
        w2s_src = w2_scales.rearrange("e s b n -> b (e s) n").bitcast(I32)
        nc.sync.dma_start(w2_codes[:, 0:4, :].bitcast(I32), w2_src[:, 0:4, :])
        for q in range(4):
            nc.sync.dma_start(w2_plane[32 * q : 32 * q + 4].bitcast(I32), w2s_src[4 * q : 4 * q + 4])
        nc.sync.dma_start(w2_codes[:, 4:8, :].bitcast(I32), w2_src[:, 4:8, :])
        pos_t = []
        for r, pos in enumerate((pos1, pos2)):
            pos_t.append(keep.tile([P, T // 16], U16, name=f"pos{r}"))
            nc.sync.dma_start(pos_t[r][:], pos)
        gate_t = keep.tile([P, 2, T - P], F32)
        nc.sync.dma_start(gate_t[:], gate[:, :, P:T].rearrange("r p t -> p r t"))
        gate_col = [keep.tile([P, TURNED // P], F32, name=f"gate_col{r}") for r in range(2)]
        with nc.allow_non_contiguous_dma(reason="one gate value a partition"):
            for r in range(2):
                nc.sync.dma_start(gate_col[r][:], gate[r, 0, 0:TURNED].rearrange("(c p) -> p c", p=P))

        w1_codes = keep.tile([P, 2 * H], U8, align_bytes=64)
        w1_plane = keep.tile([P, H], U8, align_bytes=64)
        h_pairs = []
        windows = []
        for a in range(2):
            js = slice(2 * a, 2 * a + 2)
            nc.vector.tensor_copy(
                w1_codes[:].bitcast(U16).rearrange("p (j m) -> p j m", j=4)[:, js, :],
                w1_raw[:].bitcast(U16).rearrange("p (m j) -> p j m", j=4)[:, js, :],
            )
            nc.vector.tensor_copy(
                w1_plane[:].rearrange("p (j m) -> p j m", j=4)[:, js, :],
                w1s_raw[:].rearrange("p (m j) -> p j m", j=4)[:, js, :],
            )
        spare = psum.tile([P, 512], F32, tag="bank7", name="bank")
        for lo, n in ((0, 256), (256, 128)):
            nc.tensor.matmul_mx(
                out=spare[:, lo : lo + n],
                lhsT=x_codes[:, 0:P].bitcast(FP8X4),
                lhsT_scale=w1s_raw[:, 0:P],
                rhs=w1_raw[:, 2 * lo : 2 * (lo + n)].bitcast(FP4X4),
                rhs_scale=w1s_raw[:, lo : lo + n],
                start=True,
                stop=True,
            )
        banks_used = 0
        planes = keep.tile([P, 2, T], BF16, name="planes")
        for a, width in enumerate((128, 256)):
            window = shared.tile([P, (WIDE, T)[a]], U32, name=f"window{a}", offset=(5120, 0)[a], align_bytes=64)
            windows.append(window[:])
            pairs = window[:, 0:T].bitcast(BF16).rearrange("p (t b) -> p t b", b=2)
            h_pairs.append(pairs)
            for t0 in range(0, T, width):
                toks = slice(t0, t0 + width)
                bank = psum.tile([P, 512], F32, tag=f"bank{banks_used}", name="bank")
                banks_used += 1
                for b in range(2):
                    j = 2 * a + b
                    nc.tensor.matmul_mx(
                        out=bank[:, b * width : (b + 1) * width],
                        lhsT=w1_codes[:, 2 * P * j : 2 * P * (j + 1)].bitcast(FP4X4),
                        lhsT_scale=w1_plane[:, P * j : P * (j + 1)],
                        rhs=x_codes[:, toks].bitcast(FP8X4),
                        rhs_scale=x_plane[:, toks],
                        start=True,
                        stop=True,
                    )
                nc.scalar.activation(pairs[:, toks, :], bank[:, 0 : 2 * width].rearrange("p (b t) -> p t b", b=2), SILU)
                if a == 0 and t0 + width < T:
                    nc.vector.tensor_copy(planes[:, :, toks], pairs[:, toks, :].rearrange("p t b -> p b t"))

        GROUPED = S + STARTS[3]
        work = keep.tile([P, GROUPED + 2 * S], U32, name="work", tag="work", align_bytes=64)
        h_codes = {}
        h_plane = keep.tile([P, S], U8, align_bytes=64)
        second_at = [S + STARTS[0], S + STARTS[1], S + STARTS[2], S, S + CHUNKS[3]]

        def slots(s0, n):
            return offs_t[:, s0 // 16 : (s0 + n) // 16]

        def gather_first(s0, n):
            nc.vector.tensor_copy(work[:, s0 : s0 + n], windows[0].indirect(slots(s0, n)))

        def gather_second(c):
            nc.vector.tensor_copy(work[:, second_at[c] : second_at[c] + CHUNKS[c]], windows[1].indirect(slots(STARTS[c], CHUNKS[c])))

        def grouped(c):
            return work[:, GROUPED + 2 * STARTS[c] : GROUPED + 2 * (STARTS[c] + CHUNKS[c])]

        def interleave(c):
            copy = nc.gpsimd.tensor_copy if c == 0 else nc.scalar.copy
            apart = second_at[c] - STARTS[c]
            both = work[:, STARTS[c] : STARTS[c] + 2 * apart].rearrange("p (a n) -> p n a", a=2)[:, 0 : CHUNKS[c], :]
            copy(grouped(c).rearrange("p (n a) -> p n a", a=2), both)

        def quantise(c):
            if c == 2:
                h_codes[c] = shared.tile([P, CHUNKS[c]], U32, name="late_codes", offset=0, align_bytes=64)
            else:
                h_codes[c] = keep.tile([P, CHUNKS[c]], U32, name=f"codes{c}", align_bytes=64)
            step = C if c == 2 else CHUNKS[c]
            for lo in range(0, CHUNKS[c], step):
                nc.vector.quantize_mx(
                    out=h_codes[c][:, lo : lo + step].bitcast(FP8X4),
                    scales=h_plane[:, STARTS[c] + lo : STARTS[c] + lo + step],
                    in_=grouped(c)[:, 2 * lo : 2 * (lo + step)].bitcast(BF16),
                )

        def experts(c, u, bank, at):
            for s in range(STARTS[c], STARTS[c] + CHUNKS[c], C):
                e = s // C
                nc.tensor.matmul_mx(
                    out=bank[:, s - at : s - at + C],
                    lhsT=w2_codes[:, e, P * u : P * (u + 1)].bitcast(FP8X4),
                    lhsT_scale=w2_plane[:, e, P * u : P * (u + 1)],
                    rhs=h_codes[c][:, s - STARTS[c] : s - STARTS[c] + C].bitcast(FP8X4),
                    rhs_scale=h_plane[:, s : s + C],
                    start=True,
                    stop=True,
                )

        gather_first(0, FIRST_PAIR)
        nc.gpsimd.tensor_copy(planes[:, :, T - P : T], h_pairs[0][:, T - P : T, :].rearrange("p t b -> p b t"))
        s0 = FIRST_PAIR
        halves = work[:, s0:S].bitcast(BF16).rearrange("p (n b) -> p n b", b=2)
        for b in range(2):
            nc.scalar.activation(halves[:, :, b], planes[:, b, :].indirect(slots(s0, S - s0)), COPY)
        for c in range(3):
            gather_second(c)
            interleave(c)
        for c in range(2):
            quantise(c)
            gather_second(3 + c)
            interleave(3 + c)
        for c in range(2, 5):
            quantise(c)

        GROUPS = ((0, 1), (2,), (3, 4))
        y = [shared.tile([P, S], F32, name="y0", offset=1024, align_bytes=64), keep.tile([P, S], F32, name="y1", tag="work", align_bytes=64)]
        banks = {}

        def products(u, g, tag):
            banks[u, g] = psum.tile([P, 512], F32, tag=tag, name="bank")
            for c in GROUPS[g]:
                experts(c, u, banks[u, g], STARTS[GROUPS[g][0]])

        def empty(u, g):
            copy = nc.vector.tensor_copy if u == 1 and g < 2 else nc.scalar.copy
            s0, n = STARTS[GROUPS[g][0]], sum(CHUNKS[c] for c in GROUPS[g])
            copy(y[u][:, s0 : s0 + n], banks[u, g][:, 0:n])

        products(0, 0, "bank6")
        products(1, 0, "bank7")
        products(0, 1, "bank0")
        products(0, 2, "bank1")
        for g in range(3):
            empty(0, g)
        products(1, 1, "bank2")
        products(1, 2, "bank3")
        for g in range(3):
            empty(1, g)

        prod = [[keep.tile([P, T], F32, name=f"prod{u}{r}") for r in range(2)] for u in range(2)]
        res = [keep.tile([P, T], F32, name=f"res{u}") for u in range(2)]
        ident = keep.tile([P, P], F32)
        make_identity(nc, ident[:])

        def tokens(r, t0, t1):
            return pos_t[r][:, t0 // 16 : t1 // 16]

        def pick(u, r, t0, t1):
            nc.vector.tensor_tensor(prod[u][r][:, t0:t1], y[u][:].indirect(tokens(r, t0, t1)), gate_t[:, r, t0 - P : t1 - P], MULT)

        def add(u, t0, t1):
            nc.vector.tensor_tensor(res[u][:, t0:t1], prod[u][0][:, t0:t1], prod[u][1][:, t0:t1], ADD)
            nc.sync.dma_start(out[P * u : P * (u + 1), t0:t1], res[u][:, t0:t1])

        SHARE = (256, 128)
        plain = [[keep.tile([P, SHARE[u]], F32, name=f"plain{u}{r}") for r in range(2)] for u in range(2)]
        weighed = [[keep.tile([P, SHARE[u]], F32, name=f"weighed{u}{r}") for r in range(2)] for u in range(2)]
        turned = {}
        back = {}

        def fetch(u, r):
            nc.scalar.activation(plain[u][r][:], y[u][:].indirect(tokens(r, 0, SHARE[u])), COPY)
            turned[u, r] = psum.tile([P, 512], F32, tag=f"bank{2 + 2 * u + r}", name="bank")
            for t0 in range(0, SHARE[u], P):
                nc.tensor.transpose(turned[u, r][:, t0 : t0 + P], plain[u][r][:, t0 : t0 + P], ident[:])

        def weigh(u, b, tag):
            blk = slice(P * b, P * (b + 1))
            back[u, b] = psum.tile([P, 512], F32, tag=tag, name="bank")
            for r in range(2):
                nc.scalar.activation(weighed[u][r][:, blk], turned[u, r][:, blk], COPY, scale=gate_col[r][:, b : b + 1])
                nc.tensor.matmul(back[u, b][:, 0:P], weighed[u][r][:, blk], ident[:], start=(r == 0), stop=(r == 1), is_transpose=True)

        def leave(u, b):
            blk = slice(P * b, P * (b + 1))
            nc.scalar.copy(res[u][:, blk], back[u, b][:, 0:P])
            nc.scalar.dma_start(out[P * u : P * (u + 1), blk], res[u][:, blk])

        fetch(0, 0)
        fetch(0, 1)
        fetch(1, 0)
        weigh(0, 0, "bank1")
        fetch(1, 1)
        leave(0, 0)
        weigh(0, 1, "bank7")
        weigh(1, 0, "bank6")
        leave(0, 1)
        leave(1, 0)

        pick(0, 0, SHARE[0], T)
        pick(0, 1, SHARE[0], T)
        pick(1, 0, P, 2 * P)
        pick(1, 1, P, 2 * P)
        add(0, SHARE[0], T)
        add(1, P, 2 * P)
        pick(1, 0, 2 * P, T)
        pick(1, 1, 2 * P, 3 * P)
        pick(1, 1, 3 * P, T)
        add(1, 2 * P, 3 * P)
        add(1, 3 * P, T)
